import numpy as np
import ml_dtypes

BF16 = ml_dtypes.bfloat16


def bf(x):
    return np.asarray(x, np.float32).astype(BF16)


def f32(x):
    return np.asarray(x, np.float32)


def f64(x):
    return np.asarray(x).astype(np.float64)


def striped(idx):
    return np.tile(idx.reshape(-1, 16).T, (8, 1))


S, K, M, N, B, Q = 256, 512, 128, 128, 2, 64


def gelu_tanh(v):
    return 0.5 * v * (1.0 + np.tanh(np.sqrt(2.0 / np.pi) * (v + 0.044715 * v**3)))


def setup_inputs():
    return {"base": bf(np.random.standard_normal((B, M, S))), "x": bf(np.random.standard_normal((K, N))), "w": bf(np.random.standard_normal((K, M)) / np.sqrt(K)), "b": f32(0.5 * np.random.standard_normal((M, 1))), "offs": striped(np.random.permutation(S)[:N])}


def reference(base, x, w, b, offs):
    idx = offs[:16].T.reshape(-1)
    z = f64(base).copy()
    for i in range(B):
        z[i][:, idx[i * Q : (i + 1) * Q]] += f64(w).T @ f64(x)[:, i * Q : (i + 1) * Q]
    return gelu_tanh(z + f64(b))

@@ -1,0 +1,58 @@
+import concourse.mybir as mybir
+from concourse.masks import make_identity
+
+BF16, F32, U16 = mybir.dt.bfloat16, mybir.dt.float32, mybir.dt.uint16
+GELU_TANH = mybir.ActivationFunctionType.Gelu_apprx_tanh
+
+P = 128
+S = 256
+K = 512
+N = 128
+B = 2
+Q = N // B
+BLOCKS = K // P
+OFFSET_ROWS = 16
+
+FLOPS = 2 * K * P * N
+
+
+def tile_scatter_matmul_kernel(tc, base, x, w, b, offs, out):
+    nc = tc.nc
+    with (
+        tc.tile_pool(name="held", bufs=1) as held,
+        tc.psum_pool(name="psum", bufs=1) as psum,
+    ):
+        offsets = held.tile([P, N // OFFSET_ROWS], U16, name="offsets")
+        base_tile = held.tile([P, B, S], BF16, name="base_tile")
+        x_tile = held.tile([P, BLOCKS, N], BF16, name="x_tile")
+        w_tile = held.tile([P, BLOCKS, P], BF16, name="w_tile")
+        bias = held.tile([P, 1], F32, name="bias")
+        ident = held.tile([P, P], BF16, name="ident")
+
+        nc.sync.dma_start(base_tile[:], base.rearrange("i m t -> m i t"))
+        nc.sync.dma_start(w_tile[:], w.rearrange("(p a) m -> p a m", a=BLOCKS))
+        nc.sync.dma_start(x_tile[:], x.rearrange("(p a) j -> p a j", a=BLOCKS))
+        nc.sync.dma_start(offsets[:], offs)
+        nc.scalar.dma_start(bias[:], b)
+        make_identity(nc, ident[:])
+
+        windows = [psum.tile([P, S], F32, name=f"window_{i}") for i in range(B)]
+        for i in range(B):
+            nc.tensor.matmul(windows[i][:], ident[:], base_tile[:, i, :], start=True, stop=False)
+
+        piece = Q // OFFSET_ROWS
+        for i in range(B):
+            places = windows[i][:].indirect(offsets[:, i * piece : (i + 1) * piece])
+            for a in range(BLOCKS):
+                nc.tensor.matmul(
+                    places,
+                    w_tile[:, a, :],
+                    x_tile[:, a, i * Q : (i + 1) * Q],
+                    start=False,
+                    stop=a == BLOCKS - 1,
+                )
+
+        for i in range(B):
+            result = held.tile([P, S], F32, name=f"result_{i}")
+            nc.scalar.activation(result[:], windows[i][:], GELU_TANH, bias=bias[:])
+            nc.sync.dma_start(out[i], result[:])

@@ -12,6 +12,7 @@ B = 2
 Q = N // B
 BLOCKS = K // P
 OFFSET_ROWS = 16
+WARM_UPS = 6
 
 FLOPS = 2 * K * P * N
 
@@ -33,8 +34,19 @@ def tile_scatter_matmul_kernel(tc, base, x, w, b, offs, out):
         nc.sync.dma_start(w_tile[:], w.rearrange("(p a) m -> p a m", a=BLOCKS))
         nc.sync.dma_start(x_tile[:], x.rearrange("(p a) j -> p a j", a=BLOCKS))
         nc.sync.dma_start(offsets[:], offs)
-        nc.scalar.dma_start(bias[:], b)
+        nc.sync.dma_start(bias[:], b)
         make_identity(nc, ident[:])
+
+        zero = held.tile([P, 1], F32, name="zero")
+        early_gelu = held.tile([P, 1], F32, name="early_gelu")
+        nc.vector.memset(zero[:], 0.0)
+        nc.scalar.activation(early_gelu[:], zero[:], GELU_TANH, bias=zero[:])
+
+        zeros = held.tile([P, S], BF16, name="zeros")
+        spare = psum.tile([P, S], F32, name="spare")
+        nc.vector.memset(zeros[:], 0.0)
+        for repeat in range(WARM_UPS):
+            nc.tensor.matmul(spare[:], zeros[:, :P], zeros[:], start=True, stop=True)
 
         windows = [psum.tile([P, S], F32, name=f"window_{i}") for i in range(B)]
         for i in range(B):

import concourse.mybir as mybir
from concourse.masks import make_identity

BF16, F32, U16 = mybir.dt.bfloat16, mybir.dt.float32, mybir.dt.uint16
GELU_TANH = mybir.ActivationFunctionType.Gelu_apprx_tanh

P = 128
S = 256
K = 512
N = 128
B = 2
Q = N // B
BLOCKS = K // P
OFFSET_ROWS = 16
WARM_UPS = 6

FLOPS = 2 * K * P * N


def tile_scatter_matmul_kernel(tc, base, x, w, b, offs, out):
    nc = tc.nc
    with (
        tc.tile_pool(name="held", bufs=1) as held,
        tc.psum_pool(name="psum", bufs=1) as psum,
    ):
        offsets = held.tile([P, N // OFFSET_ROWS], U16, name="offsets")
        base_tile = held.tile([P, B, S], BF16, name="base_tile")
        x_tile = held.tile([P, BLOCKS, N], BF16, name="x_tile")
        w_tile = held.tile([P, BLOCKS, P], BF16, name="w_tile")
        bias = held.tile([P, 1], F32, name="bias")
        ident = held.tile([P, P], BF16, name="ident")

        nc.sync.dma_start(base_tile[:], base.rearrange("i m t -> m i t"))
        nc.sync.dma_start(w_tile[:], w.rearrange("(p a) m -> p a m", a=BLOCKS))
        nc.sync.dma_start(x_tile[:], x.rearrange("(p a) j -> p a j", a=BLOCKS))
        nc.sync.dma_start(offsets[:], offs)
        nc.sync.dma_start(bias[:], b)
        make_identity(nc, ident[:])

        zero = held.tile([P, 1], F32, name="zero")
        early_gelu = held.tile([P, 1], F32, name="early_gelu")
        nc.vector.memset(zero[:], 0.0)
        nc.scalar.activation(early_gelu[:], zero[:], GELU_TANH, bias=zero[:])

        zeros = held.tile([P, S], BF16, name="zeros")
        spare = psum.tile([P, S], F32, name="spare")
        nc.vector.memset(zeros[:], 0.0)
        for repeat in range(WARM_UPS):
            nc.tensor.matmul(spare[:], zeros[:, :P], zeros[:], start=True, stop=True)

        windows = [psum.tile([P, S], F32, name=f"window_{i}") for i in range(B)]
        for i in range(B):
            nc.tensor.matmul(windows[i][:], ident[:], base_tile[:, i, :], start=True, stop=False)

        piece = Q // OFFSET_ROWS
        for i in range(B):
            places = windows[i][:].indirect(offsets[:, i * piece : (i + 1) * piece])
            for a in range(BLOCKS):
                nc.tensor.matmul(
                    places,
                    w_tile[:, a, :],
                    x_tile[:, a, i * Q : (i + 1) * Q],
                    start=False,
                    stop=a == BLOCKS - 1,
                )

        for i in range(B):
            result = held.tile([P, S], F32, name=f"result_{i}")
            nc.scalar.activation(result[:], windows[i][:], GELU_TANH, bias=bias[:])
            nc.sync.dma_start(out[i], result[:])
